import numpy as np, ml_dtypes
CORES = [3,5,19,21,35,37,51,53,67,69]
N = 10
import mx_ref
NC, ROOT = 384, 7
C = np.float32(0.043)
BF = ml_dtypes.bfloat16
def cut(t, i, w=512):
    return t[:, w * i:w * i + w]
def tile(rs):
    return np.stack(rs, axis=2).reshape(128, -1).astype(BF)
def pick(b):
    s = np.zeros((128, 128, 4), np.float32)
    s[np.arange(128), np.arange(128), b] = 1.0
    return mx_ref.quantize(s.reshape(128, 512).astype(BF))
def pk(c, s, i=0):
    return (np.ascontiguousarray(c[:, 512 * i:512 * i + 512]), mx_ref.live(s[:, 128 * i:128 * i + 128]))
def inputs(rng, e, E):
    def f(*shape):
        v = (rng.standard_normal(shape, dtype=np.float32) * np.exp2(rng.integers(-2, 3, shape[:-1] + (1,)))).astype(BF)
        return mx_ref.spread((v.astype(np.float32) * np.exp2(rng.integers(-E, E + 1, shape[:-2] + (1, 1))).astype(np.float32)).astype(BF), rng, e)
    def packed(k):
        c = np.zeros((N, 128, k * 512), np.uint8); s = np.zeros((N, 128, k * 128), np.uint8)
        for r in range(N):
            for i in range(k):
                a, b = mx_ref.quantize(f(128, 512)); c[r][:, 512 * i:512 * i + 512] = a; s[r][:, 128 * i:128 * i + 128] = mx_ref.plane(b, rng)
        return c, s
    d = {}
    d["wc"], d["ws"] = packed(1)
    d["a"] = f(N, 128, 512)
    d["bb"] = f(N, 128, 4 * 512)
    d["x"] = f(N, 128, 4 * NC)
    return d
def setup_inputs(rng):
    return inputs(rng, 0, 0)
def setup_inputs_blocks(rng):
    return inputs(rng, 2, 0)
def setup_inputs_wide(rng):
    return inputs(rng, 0, 3)
def reference(wc, ws, a, bb, x):
    S = [pick(t) for t in range(4)]; A = mx_ref.quantize(a[ROOT])
    V = [mx_ref.quantize(tile([mx_ref.matmul(S[t], pk(wc[j], ws[j])) + mx_ref.matmul(mx_ref.quantize(cut(bb[j], t)), A) * C for t in range(4)])) for j in range(N)]
    y = np.zeros((N, 128, N * NC), np.float32)
    for r in range(N):
        X = mx_ref.quantize(x[r])
        for j in range(N):
            y[r][:, NC * j:NC * j + NC] = mx_ref.matmul(V[j], X)
    return {"y": y}

@@ -1,0 +1,194 @@
+from concourse.bass import DstId, RemoteDMATransfer
+from concourse.mybir import dt, AluOpType, ActivationFunctionType
+
+NT, NX, N = 128, 384, 10
+C = 0.043
+OFF = 4
+OWN, FWD, MATE = OFF, OFF + 1, 2 * OFF + 1
+F8, U8, BF, F32 = "float8_e4m3fn_x4", "uint8", "bfloat16", "float32"
+
+SCRATCH = {
+    "ta": ("sbuf", [128, 4 * NT], BF),
+    "tb": ("sbuf", [128, 16 * NT], BF),
+    "tx": ("sbuf", [128, 4 * NX], BF),
+    "ones": ("sbuf", [128, 4 * NT + 4], BF),
+    "diag": ("sbuf", [128, 4 * NT + 4], BF),
+    "tmp": ("sbuf", [128, 4 * NT], F32),
+    "tv": ("sbuf", [128, 4 * NT], BF),
+    "ysb": ("sbuf", [128, N * NX], F32),
+    "ac": ("sbuf", [128, NT], F8), "ap": ("sbuf", [128, NT], U8),
+    "bc": ("sbuf", [128, 4 * NT], F8), "bp": ("sbuf", [128, 4 * NT], U8),
+    "xc": ("sbuf", [128, NX], F8), "xp": ("sbuf", [128, NX], U8),
+    "sc": ("sbuf", [128, 4 * NT], F8), "sp": ("sbuf", [128, 4 * NT], U8),
+    "wqc": ("sbuf", [128, NT], F8), "wqp": ("sbuf", [128, NT], U8),
+    "vc": ("sbuf", [128, N * NT], F8), "vp": ("sbuf", [128, N * NT], U8),
+    "pd": ("psum", [128, 2048], F32),
+    "pm": ("psum", [128, 2048], F32),
+}
+SEMAPHORES = ["la", "lb", "lx", "lw", "one", "dia", "qa", "qb", "qs", "qx", "dd", "mm", "ml", "ad", "qv", "sent",
+              "rac", "rap", "rm", "rf", "my", "cv", "ca", "st", "ss"] + ["r%d" % i for i in range(OFF + 1)]
+
+
+def _bits(m):
+    return bin(m).count("1")
+
+
+def rank_program(g, core, T, topo):
+    if T.rank_of(core) is None:
+        return
+    S = T.sem
+    cores = list(T.cores)
+    chips = sorted(set(topo.chip(c) for c in cores))
+
+    def at(k, die):
+        ch = chips[k % len(chips)]
+        return [c for c in cores if topo.chip(c) == ch and topo.die(c) == die][0]
+
+    k = chips.index(topo.chip(core))
+    die = topo.die(core)
+    root = cores[T.root]
+    is_root = core == root
+    mate = [c for c in cores if topo.chip(c) == topo.chip(core) and c != core][0]
+    peers = [at(k + 1 + i, die) for i in range(OFF)]
+    cross = [at(k + 1 + i, topo.die(mate)) for i in range(OFF)]
+    off = topo.mask(core, peers[0])
+    on = topo.mask(core, mate)
+    rest = on & ~off
+    sent = [0]
+
+    def slot_at(dst):
+        return (k - chips.index(topo.chip(dst)) - 1) % len(chips)
+
+    def send(src, dsts, mask, sem):
+        ids = []
+        for c, _ in dsts:
+            rid, pid, _e = topo.addr(c)
+            ids.append(DstId(rid=rid, pnc=pid))
+        g.remote_dma_fused([RemoteDMATransfer(dst_ids=ids, dma_engine_mask=mask, remote_sem=sem, srcs=[src],
+                                              dsts=[d for _, d in dsts])], local_sem=S.sent)
+        sent[0] += _bits(mask)
+
+    def vcod(a, n=1):
+        return T.vc[:, a * NT:(a + n) * NT].bitcast(dt.uint8)
+
+    def vpln(a, n=1):
+        return T.vp[:, a * NT:(a + n) * NT]
+
+    acod = T.ac[:].bitcast(dt.uint8)
+    apln = T.ap[:]
+
+    if is_root:
+        g.sync.dma_start(T.ta[:], T.a[:]).then_inc(S.la, 16)
+    q = g.sync if is_root else g.scalar
+    q.dma_start(T.wqc[:].bitcast(dt.uint8), T.wc[:]).then_inc(S.lw, 16)
+    q.dma_start(T.wqp[:], T.ws[:]).then_inc(S.lw, 16)
+    g.sync.dma_start(T.tb[:], T.bb[:]).then_inc(S.lb, 16)
+    q.dma_start(T.tx[:], T.x[:]).then_inc(S.lx, 16)
+
+    g.vector.memset(T.ones[:], 1.0).then_inc(S.one, 1)
+    if is_root:
+        g.vector.wait_ge(S.la, 16)
+        g.vector.quantize_mx(T.ac[:], T.ap[:], T.ta[:]).then_inc(S.qa, 1)
+    g.vector.wait_ge(S.dia, 1)
+    for b in range(4):
+        g.vector.quantize_mx(T.sc[:, b * NT:(b + 1) * NT], T.sp[:, b * NT:(b + 1) * NT],
+                             T.diag[:, 3 - b:3 - b + 4 * NT]).then_inc(S.qs, 1)
+    g.vector.wait_ge(S.lb, 16)
+    g.vector.quantize_mx(T.bc[:], T.bp[:], T.tb[:]).then_inc(S.qb, 1)
+    g.vector.wait_ge(S.lx, 16)
+    g.vector.quantize_mx(T.xc[:], T.xp[:], T.tx[:]).then_inc(S.qx, 1)
+
+    def diagonal():
+        g.wait_ge(S.one, 1)
+        g.affine_select(T.diag[:], T.ones[:], [[-1, 4 * NT + 4]], AluOpType.is_equal, 0.0, 3, 4).then_inc(S.dia, 1)
+
+    if is_root:
+        g.wait_ge(S.qa, 1)
+        send(acod, [(c, acod) for c in peers], off, S.rac)
+        send(apln, [(c, apln) for c in cross], off, S.rap)
+        send(acod, [(mate, acod)], rest, S.rac)
+        send(apln, [(mate, apln)], rest, S.rap)
+        diagonal()
+    else:
+        diagonal()
+        if mate != root:
+            if die == topo.die(root):
+                g.wait_ge(S.rac, _bits(off))
+                send(acod, [(mate, acod)], off, S.rac)
+            else:
+                g.wait_ge(S.rap, _bits(off))
+                send(apln, [(mate, apln)], off, S.rap)
+
+    g.tensor.wait_ge(S.lw, 32)
+    g.tensor.wait_ge(S.qs, 4)
+    for b in range(4):
+        g.tensor.matmul_mx(T.pd[:, 512 * b:512 * b + NT], T.sc[:, b * NT:(b + 1) * NT], T.sp[:, b * NT:(b + 1) * NT],
+                           T.wqc[:], T.wqp[:], True, True).then_inc(S.dd, 1)
+    g.tensor.wait_ge(S.qb, 1)
+    g.tensor.wait_ge(S.qx, 1)
+    if is_root:
+        g.tensor.wait_ge(S.qa, 1)
+    else:
+        n = _bits(rest) if mate == root else _bits(off)
+        g.tensor.wait_ge(S.rac, n)
+        g.tensor.wait_ge(S.rap, n)
+    for b in range(4):
+        g.tensor.matmul_mx(T.pm[:, 512 * b:512 * b + NT], T.bc[:, b * NT:(b + 1) * NT], T.bp[:, b * NT:(b + 1) * NT],
+                           T.ac[:], T.ap[:], True, True).then_inc(S.mm, 1)
+
+    g.vector.wait_ge(S.dd, 4)
+    for b in range(4):
+        g.scalar.wait_ge(S.mm, b + 1)
+        g.scalar.activation(T.tmp[:, b * NT:(b + 1) * NT], T.pm[:, 512 * b:512 * b + NT],
+                            ActivationFunctionType.Copy, scale=C).then_inc(S.ml, 1)
+        g.vector.wait_ge(S.ml, b + 1)
+        g.vector.tensor_tensor(T.tv[:, b:4 * NT:4], T.tmp[:, b * NT:(b + 1) * NT], T.pd[:, 512 * b:512 * b + NT],
+                               AluOpType.add).then_inc(S.ad, 1)
+    g.vector.wait_ge(S.ad, 4)
+    g.vector.quantize_mx(T.vc[:, OWN * NT:(OWN + 1) * NT], T.vp[:, OWN * NT:(OWN + 1) * NT], T.tv[:]).then_inc(S.qv, 1)
+
+    g.wait_ge(S.qv, 1)
+    for half in (vcod, vpln):
+        send(half(OWN), [(c, half(slot_at(c))) for c in peers], off, S["r%d" % k])
+    send(vcod(OWN), [(mate, vcod(MATE))], rest, S.rm)
+    send(vpln(OWN), [(mate, vpln(MATE))], rest, S.rm)
+    came = [S["r%d" % ((k + 1 + i) % len(chips))] for i in range(OFF)]
+    for i in range(OFF):
+        g.wait_ge(came[i], 2 * _bits(off))
+    send(vcod(0, OFF), [(mate, vcod(FWD, OFF))], on, S.rf)
+    send(vpln(0, OFF), [(mate, vpln(FWD, OFF))], on, S.rf)
+
+    order = [(OWN, core, S.qv, 1), (MATE, mate, S.rm, 2 * _bits(rest))]
+    order += [(i, peers[i], came[i], 2 * _bits(off)) for i in range(OFF)]
+    order += [(FWD + i, cross[i], S.rf, 2 * _bits(on)) for i in range(OFF)]
+    nv = na = nst = nss = 0
+    for n, (slot, src, sem, cnt) in enumerate(order):
+        j = T.rank_of(src)
+        bank = (T.pm if n % 8 < 4 else T.pd)[:, 512 * (n % 4):512 * (n % 4) + NX]
+        if n >= 8:
+            g.tensor.wait_ge(S.cv if n % 2 == 0 else S.ca, (n - 8) // 2 + 1)
+        g.tensor.wait_ge(sem, cnt)
+        g.tensor.matmul_mx(bank, T.vc[:, slot * NT:(slot + 1) * NT], T.vp[:, slot * NT:(slot + 1) * NT],
+                           T.xc[:], T.xp[:], True, True).then_inc(S.my, 1)
+        dst = T.ysb[:, NX * j:NX * (j + 1)]
+        if n % 2 == 0:
+            g.vector.wait_ge(S.my, n + 1)
+            g.vector.tensor_copy(dst, bank).then_inc(S.cv, 1)
+            nv += 1
+            done = (S.cv, nv)
+        else:
+            g.scalar.wait_ge(S.my, n + 1)
+            g.scalar.activation(dst, bank, ActivationFunctionType.Copy).then_inc(S.ca, 1)
+            na += 1
+            done = (S.ca, na)
+        if n == N - 1:
+            g.scalar.wait_ge(*done)
+            g.scalar.dma_start(T.y[:, NX * j:NX * (j + 1)], dst).then_inc(S.ss, 16)
+            nss += 16
+        else:
+            g.sync.wait_ge(*done)
+            g.sync.dma_start(T.y[:, NX * j:NX * (j + 1)], dst).then_inc(S.st, 16)
+            nst += 16
+    g.scalar.wait_ge(S.ss, nss)
+    g.sync.wait_ge(S.st, nst)
+    g.wait_ge(S.sent, sent[0])

@@ -11,7 +11,8 @@ SCRATCH = {
     "ta": ("sbuf", [128, 4 * NT], BF),
     "tb": ("sbuf", [128, 16 * NT], BF),
     "tx": ("sbuf", [128, 4 * NX], BF),
-    "ones": ("sbuf", [128, 4 * NT + 4], BF),
+    "ones": ("sbuf", [128, NT], BF),
+    "eye": ("sbuf", [128, NT], BF),
     "diag": ("sbuf", [128, 4 * NT + 4], BF),
     "tmp": ("sbuf", [128, 4 * NT], F32),
     "tv": ("sbuf", [128, 4 * NT], BF),
@@ -25,8 +26,9 @@ SCRATCH = {
     "pd": ("psum", [128, 2048], F32),
     "pm": ("psum", [128, 2048], F32),
 }
-SEMAPHORES = ["la", "lb", "lx", "lw", "one", "dia", "qa", "qb", "qs", "qx", "dd", "mm", "ml", "ad", "qv", "sent",
-              "rac", "rap", "rm", "rf", "my", "cv", "ca", "st", "ss"] + ["r%d" % i for i in range(OFF + 1)]
+SEMAPHORES = ["la", "lb", "lx", "lw", "one", "zero", "dia", "cp", "qa", "qb", "qs", "qt", "qx", "dd", "mm", "ml", "ad",
+              "qv", "sent", "sa", "rs", "rac", "rap", "rm", "rf", "my", "cv", "ca", "st", "ss"]
+SEMAPHORES += ["%s%d" % (s, i) for s in ("rc", "rp") for i in range(OFF + 1)]
 
 
 def _bits(m):
@@ -54,19 +56,23 @@ def rank_program(g, core, T, topo):
     off = topo.mask(core, peers[0])
     on = topo.mask(core, mate)
     rest = on & ~off
+    ne, nr, nn = _bits(off), _bits(rest), _bits(on)
+    give = (3, 4) if die == topo.die(root) else (0, 2)
+    keep = 2
     sent = [0]
 
     def slot_at(dst):
         return (k - chips.index(topo.chip(dst)) - 1) % len(chips)
 
-    def send(src, dsts, mask, sem):
+    def send(src, dsts, mask, sem, gone=None):
         ids = []
         for c, _ in dsts:
             rid, pid, _e = topo.addr(c)
             ids.append(DstId(rid=rid, pnc=pid))
         g.remote_dma_fused([RemoteDMATransfer(dst_ids=ids, dma_engine_mask=mask, remote_sem=sem, srcs=[src],
-                                              dsts=[d for _, d in dsts])], local_sem=S.sent)
-        sent[0] += _bits(mask)
+                                              dsts=[d for _, d in dsts])], local_sem=gone or S.sent)
+        if not gone:
+            sent[0] += _bits(mask)
 
     def vcod(a, n=1):
         return T.vc[:, a * NT:(a + n) * NT].bitcast(dt.uint8)
@@ -83,55 +89,66 @@ def rank_program(g, core, T, topo):
     q.dma_start(T.wqc[:].bitcast(dt.uint8), T.wc[:]).then_inc(S.lw, 16)
     q.dma_start(T.wqp[:], T.ws[:]).then_inc(S.lw, 16)
     g.sync.dma_start(T.tb[:], T.bb[:]).then_inc(S.lb, 16)
-    q.dma_start(T.tx[:], T.x[:]).then_inc(S.lx, 16)
+    if is_root:
+        g.sync.wait_ge(S.sa, 2 * ne)
+    g.sync.dma_start(T.tx[:], T.x[:]).then_inc(S.lx, 16)
 
     g.vector.memset(T.ones[:], 1.0).then_inc(S.one, 1)
+    g.vector.memset(T.diag[:], 0.0).then_inc(S.zero, 1)
+    g.wait_ge(S.one, 1)
+    g.affine_select(T.eye[:], T.ones[:], [[-1, NT]], AluOpType.is_equal, 0.0, 0, 1).then_inc(S.dia, 1)
+    g.vector.wait_ge(S.zero, 1)
+    g.vector.wait_ge(S.dia, 1)
+    g.vector.tensor_copy(T.diag[:, 3:4 * NT:4], T.eye[:]).then_inc(S.cp, 1)
+    g.vector.wait_ge(S.cp, 1)
+
+    def pick(b, sem):
+        g.vector.quantize_mx(T.sc[:, b * NT:(b + 1) * NT], T.sp[:, b * NT:(b + 1) * NT],
+                             T.diag[:, 3 - b:3 - b + 4 * NT]).then_inc(sem, 1)
+
+    for b in range(*give):
+        pick(b, S.qs)
+    ngive = give[1] - give[0]
+    mine = slice(give[0] * NT, give[1] * NT)
+
     if is_root:
         g.vector.wait_ge(S.la, 16)
         g.vector.quantize_mx(T.ac[:], T.ap[:], T.ta[:]).then_inc(S.qa, 1)
-    g.vector.wait_ge(S.dia, 1)
-    for b in range(4):
-        g.vector.quantize_mx(T.sc[:, b * NT:(b + 1) * NT], T.sp[:, b * NT:(b + 1) * NT],
-                             T.diag[:, 3 - b:3 - b + 4 * NT]).then_inc(S.qs, 1)
+    pick(keep, S.qt)
     g.vector.wait_ge(S.lb, 16)
     g.vector.quantize_mx(T.bc[:], T.bp[:], T.tb[:]).then_inc(S.qb, 1)
-    g.vector.wait_ge(S.lx, 16)
-    g.vector.quantize_mx(T.xc[:], T.xp[:], T.tx[:]).then_inc(S.qx, 1)
 
-    def diagonal():
-        g.wait_ge(S.one, 1)
-        g.affine_select(T.diag[:], T.ones[:], [[-1, 4 * NT + 4]], AluOpType.is_equal, 0.0, 3, 4).then_inc(S.dia, 1)
-
+    g.wait_ge(S.qs, ngive)
+    scod = (T.sc[:, mine].bitcast(dt.uint8), [(mate, T.sc[:, mine].bitcast(dt.uint8))])
+    spln = (T.sp[:, mine], [(mate, T.sp[:, mine])])
     if is_root:
+        send(*spln, off, S.rs)
         g.wait_ge(S.qa, 1)
-        send(acod, [(c, acod) for c in peers], off, S.rac)
-        send(apln, [(c, apln) for c in cross], off, S.rap)
+        send(acod, [(c, acod) for c in peers], off, S.rac, S.sa)
+        send(apln, [(c, apln) for c in peers + cross], off, S.rap, S.sa)
         send(acod, [(mate, acod)], rest, S.rac)
         send(apln, [(mate, apln)], rest, S.rap)
-        diagonal()
+        send(*scod, rest, S.rs)
     else:
-        diagonal()
-        if mate != root:
-            if die == topo.die(root):
-                g.wait_ge(S.rac, _bits(off))
-                send(acod, [(mate, acod)], off, S.rac)
-            else:
-                g.wait_ge(S.rap, _bits(off))
-                send(apln, [(mate, apln)], off, S.rap)
+        send(*scod, on, S.rs)
+        send(*spln, on, S.rs)
+        if mate != root and die == topo.die(root):
+            g.wait_ge(S.rac, ne)
+            send(acod, [(mate, acod)], on, S.rac)
 
     g.tensor.wait_ge(S.lw, 32)
-    g.tensor.wait_ge(S.qs, 4)
+    g.tensor.wait_ge(S.qs, ngive)
+    g.tensor.wait_ge(S.qt, 1)
+    g.tensor.wait_ge(S.rs, ne + nr if mate == root else 2 * nn)
     for b in range(4):
         g.tensor.matmul_mx(T.pd[:, 512 * b:512 * b + NT], T.sc[:, b * NT:(b + 1) * NT], T.sp[:, b * NT:(b + 1) * NT],
                            T.wqc[:], T.wqp[:], True, True).then_inc(S.dd, 1)
     g.tensor.wait_ge(S.qb, 1)
-    g.tensor.wait_ge(S.qx, 1)
     if is_root:
         g.tensor.wait_ge(S.qa, 1)
     else:
-        n = _bits(rest) if mate == root else _bits(off)
-        g.tensor.wait_ge(S.rac, n)
-        g.tensor.wait_ge(S.rap, n)
+        g.tensor.wait_ge(S.rap, nr if mate == root else ne)
+        g.tensor.wait_ge(S.rac, nr if mate == root else ne if die == topo.die(root) else nn)
     for b in range(4):
         g.tensor.matmul_mx(T.pm[:, 512 * b:512 * b + NT], T.bc[:, b * NT:(b + 1) * NT], T.bp[:, b * NT:(b + 1) * NT],
                            T.ac[:], T.ap[:], True, True).then_inc(S.mm, 1)
@@ -146,28 +163,34 @@ def rank_program(g, core, T, topo):
                                AluOpType.add).then_inc(S.ad, 1)
     g.vector.wait_ge(S.ad, 4)
     g.vector.quantize_mx(T.vc[:, OWN * NT:(OWN + 1) * NT], T.vp[:, OWN * NT:(OWN + 1) * NT], T.tv[:]).then_inc(S.qv, 1)
+    g.vector.wait_ge(S.lx, 16)
+    g.vector.quantize_mx(T.xc[:], T.xp[:], T.tx[:]).then_inc(S.qx, 1)
 
     g.wait_ge(S.qv, 1)
-    for half in (vcod, vpln):
-        send(half(OWN), [(c, half(slot_at(c))) for c in peers], off, S["r%d" % k])
+    send(vcod(OWN), [(c, vcod(slot_at(c))) for c in peers], off, S["rc%d" % k])
+    send(vpln(OWN), [(c, vpln(slot_at(c))) for c in peers], off, S["rp%d" % k])
     send(vcod(OWN), [(mate, vcod(MATE))], rest, S.rm)
     send(vpln(OWN), [(mate, vpln(MATE))], rest, S.rm)
-    came = [S["r%d" % ((k + 1 + i) % len(chips))] for i in range(OFF)]
+    far = [(k + 1 + i) % len(chips) for i in range(OFF)]
     for i in range(OFF):
-        g.wait_ge(came[i], 2 * _bits(off))
+        g.wait_ge(S["rc%d" % far[i]], ne)
     send(vcod(0, OFF), [(mate, vcod(FWD, OFF))], on, S.rf)
+    for i in range(OFF):
+        g.wait_ge(S["rp%d" % far[i]], ne)
     send(vpln(0, OFF), [(mate, vpln(FWD, OFF))], on, S.rf)
 
-    order = [(OWN, core, S.qv, 1), (MATE, mate, S.rm, 2 * _bits(rest))]
-    order += [(i, peers[i], came[i], 2 * _bits(off)) for i in range(OFF)]
-    order += [(FWD + i, cross[i], S.rf, 2 * _bits(on)) for i in range(OFF)]
+    g.tensor.wait_ge(S.qx, 1)
+    order = [(OWN, core, [(S.qv, 1)]), (MATE, mate, [(S.rm, 2 * nr)])]
+    order += [(i, peers[i], [(S["rc%d" % far[i]], ne), (S["rp%d" % far[i]], ne)]) for i in range(OFF)]
+    order += [(FWD + i, cross[i], [(S.rf, 2 * nn)]) for i in range(OFF)]
     nv = na = nst = nss = 0
-    for n, (slot, src, sem, cnt) in enumerate(order):
+    for n, (slot, src, sems) in enumerate(order):
         j = T.rank_of(src)
         bank = (T.pm if n % 8 < 4 else T.pd)[:, 512 * (n % 4):512 * (n % 4) + NX]
         if n >= 8:
             g.tensor.wait_ge(S.cv if n % 2 == 0 else S.ca, (n - 8) // 2 + 1)
-        g.tensor.wait_ge(sem, cnt)
+        for s, v in sems:
+            g.tensor.wait_ge(s, v)
         g.tensor.matmul_mx(bank, T.vc[:, slot * NT:(slot + 1) * NT], T.vp[:, slot * NT:(slot + 1) * NT],
                            T.xc[:], T.xp[:], True, True).then_inc(S.my, 1)
         dst = T.ysb[:, NX * j:NX * (j + 1)]
@@ -192,3 +215,5 @@ def rank_program(g, core, T, topo):
     g.scalar.wait_ge(S.ss, nss)
     g.sync.wait_ge(S.st, nst)
     g.wait_ge(S.sent, sent[0])
+    if is_root:
+        g.wait_ge(S.sa, 2 * ne)

@@ -4,7 +4,10 @@ from concourse.mybir import dt, AluOpType, ActivationFunctionType
 NT, NX, N = 128, 384, 10
 C = 0.043
 OFF = 4
+NEAR = 2
 OWN, FWD, MATE = OFF, OFF + 1, 2 * OFF + 1
+GROUPS = [(OFF - NEAR, NEAR), (0, OFF - NEAR)]
+GIVE_ROOT, GIVE_OTHER, GIVE_HELPER, KEEP = 3, 0, 1, 2
 F8, U8, BF, F32 = "float8_e4m3fn_x4", "uint8", "bfloat16", "float32"
 
 SCRATCH = {
@@ -27,8 +30,8 @@ SCRATCH = {
     "pm": ("psum", [128, 2048], F32),
 }
 SEMAPHORES = ["la", "lb", "lx", "lw", "one", "zero", "dia", "cp", "qa", "qb", "qs", "qt", "qx", "dd", "mm", "ml", "ad",
-              "qv", "sent", "sa", "rs", "rac", "rap", "rm", "rf", "my", "cv", "ca", "st", "ss"]
-SEMAPHORES += ["%s%d" % (s, i) for s in ("rc", "rp") for i in range(OFF + 1)]
+              "qv", "sent", "rs", "rac", "rap", "rmc", "rmp", "rf0", "rf1", "my", "cv", "ca", "st", "ss"]
+SEMAPHORES += ["%s%d" % (s, j) for s in ("rc", "rp") for j in range(N)]
 
 
 def _bits(m):
@@ -36,43 +39,52 @@ def _bits(m):
 
 
 def rank_program(g, core, T, topo):
-    if T.rank_of(core) is None:
-        return
     S = T.sem
     cores = list(T.cores)
     chips = sorted(set(topo.chip(c) for c in cores))
+    if topo.chip(core) not in chips:
+        return
 
     def at(k, die):
         ch = chips[k % len(chips)]
         return [c for c in cores if topo.chip(c) == ch and topo.die(c) == die][0]
 
+    def helper(c):
+        return [h for h in range(topo.CHIPS * topo.CORES_PER_CHIP)
+                if topo.chip(h) == topo.chip(c) and topo.die(h) == topo.die(c) and h not in cores][0]
+
     k = chips.index(topo.chip(core))
     die = topo.die(core)
+    me = at(k, die)
+    if core != me and core != helper(me):
+        return
     root = cores[T.root]
     is_root = core == root
-    mate = [c for c in cores if topo.chip(c) == topo.chip(core) and c != core][0]
+    mate = [c for c in cores if topo.chip(c) == topo.chip(core) and c != me][0]
     peers = [at(k + 1 + i, die) for i in range(OFF)]
     cross = [at(k + 1 + i, topo.die(mate)) for i in range(OFF)]
     off = topo.mask(core, peers[0])
     on = topo.mask(core, mate)
     rest = on & ~off
     ne, nr, nn = _bits(off), _bits(rest), _bits(on)
-    give = (3, 4) if die == topo.die(root) else (0, 2)
-    keep = 2
+    from_root = (k - chips.index(topo.chip(root))) % len(chips)
     sent = [0]
 
-    def slot_at(dst):
-        return (k - chips.index(topo.chip(dst)) - 1) % len(chips)
+    def slot_at(c, dst):
+        i = (chips.index(topo.chip(c)) - chips.index(topo.chip(dst)) - 1) % len(chips)
+        return i if topo.die(c) == topo.die(dst) else FWD + i
 
-    def send(src, dsts, mask, sem, gone=None):
-        ids = []
-        for c, _ in dsts:
-            rid, pid, _e = topo.addr(c)
-            ids.append(DstId(rid=rid, pnc=pid))
-        g.remote_dma_fused([RemoteDMATransfer(dst_ids=ids, dma_engine_mask=mask, remote_sem=sem, srcs=[src],
-                                              dsts=[d for _, d in dsts])], local_sem=gone or S.sent)
-        if not gone:
+    def send(*parts):
+        transfers = []
+        for src, dsts, mask, sem in parts:
+            ids = []
+            for c, _ in dsts:
+                rid, pid, _e = topo.addr(c)
+                ids.append(DstId(rid=rid, pnc=pid))
+            transfers.append(RemoteDMATransfer(dst_ids=ids, dma_engine_mask=mask, remote_sem=sem, srcs=[src],
+                                               dsts=[d for _, d in dsts]))
             sent[0] += _bits(mask)
+        g.remote_dma_fused(transfers, local_sem=S.sent)
 
     def vcod(a, n=1):
         return T.vc[:, a * NT:(a + n) * NT].bitcast(dt.uint8)
@@ -80,18 +92,23 @@ def rank_program(g, core, T, topo):
     def vpln(a, n=1):
         return T.vp[:, a * NT:(a + n) * NT]
 
+    def to(view, cs):
+        return [(c, view(slot_at(me, c))) for c in cs]
+
     acod = T.ac[:].bitcast(dt.uint8)
     apln = T.ap[:]
+    rc, rp = S["rc%d" % T.rank_of(me)], S["rp%d" % T.rank_of(me)]
 
-    if is_root:
-        g.sync.dma_start(T.ta[:], T.a[:]).then_inc(S.la, 16)
-    q = g.sync if is_root else g.scalar
-    q.dma_start(T.wqc[:].bitcast(dt.uint8), T.wc[:]).then_inc(S.lw, 16)
-    q.dma_start(T.wqp[:], T.ws[:]).then_inc(S.lw, 16)
-    g.sync.dma_start(T.tb[:], T.bb[:]).then_inc(S.lb, 16)
-    if is_root:
-        g.sync.wait_ge(S.sa, 2 * ne)
-    g.sync.dma_start(T.tx[:], T.x[:]).then_inc(S.lx, 16)
+    if core == me:
+        if is_root:
+            g.sync.dma_start(T.ta[:], T.a[:]).then_inc(S.la, 16)
+        q = g.sync if is_root else g.scalar
+        q.dma_start(T.wqc[:].bitcast(dt.uint8), T.wc[:]).then_inc(S.lw, 16)
+        q.dma_start(T.wqp[:], T.ws[:]).then_inc(S.lw, 16)
+        g.sync.dma_start(T.tb[:], T.bb[:]).then_inc(S.lb, 16)
+        if is_root:
+            g.sync.wait_ge(S.qb, 1)
+        g.sync.dma_start(T.tx[:], T.x[:]).then_inc(S.lx, 16)
 
     g.vector.memset(T.ones[:], 1.0).then_inc(S.one, 1)
     g.vector.memset(T.diag[:], 0.0).then_inc(S.zero, 1)
@@ -106,52 +123,80 @@ def rank_program(g, core, T, topo):
         g.vector.quantize_mx(T.sc[:, b * NT:(b + 1) * NT], T.sp[:, b * NT:(b + 1) * NT],
                              T.diag[:, 3 - b:3 - b + 4 * NT]).then_inc(sem, 1)
 
-    for b in range(*give):
-        pick(b, S.qs)
-    ngive = give[1] - give[0]
-    mine = slice(give[0] * NT, give[1] * NT)
+    give = GIVE_HELPER if core != me else GIVE_ROOT if die == topo.die(root) else GIVE_OTHER
+    taker = me if core != me else mate
+    pick(give, S.qs)
+    mine = slice(give * NT, (give + 1) * NT)
+    scod = (T.sc[:, mine].bitcast(dt.uint8), [(taker, T.sc[:, mine].bitcast(dt.uint8))])
+    spln = (T.sp[:, mine], [(taker, T.sp[:, mine])])
+    g.wait_ge(S.qs, 1)
+
+    if core != me:
+        send((*scod, off, S.rs))
+        send((*spln, off, S.rs))
+        if not from_root:
+            g.wait_ge(S.rap, ne)
+            send((apln, [(c, apln) for c in peers], off, S.rap))
+        g.wait_ge(S.rmc, nr)
+        send((vcod(OWN), to(vcod, peers[NEAR:]), off, rc))
+        g.wait_ge(S.rmp, nr)
+        send((vpln(OWN), to(vpln, peers[NEAR:]), off, rp))
+        g.wait_ge(S.sent, sent[0])
+        return
 
     if is_root:
         g.vector.wait_ge(S.la, 16)
         g.vector.quantize_mx(T.ac[:], T.ap[:], T.ta[:]).then_inc(S.qa, 1)
-    pick(keep, S.qt)
+    pick(KEEP, S.qt)
     g.vector.wait_ge(S.lb, 16)
     g.vector.quantize_mx(T.bc[:], T.bp[:], T.tb[:]).then_inc(S.qb, 1)
 
-    g.wait_ge(S.qs, ngive)
-    scod = (T.sc[:, mine].bitcast(dt.uint8), [(mate, T.sc[:, mine].bitcast(dt.uint8))])
-    spln = (T.sp[:, mine], [(mate, T.sp[:, mine])])
+    acs = aps = 0
     if is_root:
-        send(*spln, off, S.rs)
+        send((*spln, off, S.rs))
         g.wait_ge(S.qa, 1)
-        send(acod, [(c, acod) for c in peers], off, S.rac, S.sa)
-        send(apln, [(c, apln) for c in peers + cross], off, S.rap, S.sa)
-        send(acod, [(mate, acod)], rest, S.rac)
-        send(apln, [(mate, apln)], rest, S.rap)
-        send(*scod, rest, S.rs)
+        send((apln, [(helper(c), apln) for c in (mate, core)], off, S.rap))
+        send((acod, [(c, acod) for c in [mate] + peers[:NEAR]], off, S.rac))
+        send((acod, [(c, acod) for c in peers[NEAR:]], off, S.rac))
+        send((apln, [(mate, apln)], rest, S.rap))
+        send((*scod, rest, S.rs))
     else:
-        send(*scod, on, S.rs)
-        send(*spln, on, S.rs)
-        if mate != root and die == topo.die(root):
-            g.wait_ge(S.rac, ne)
-            send(acod, [(mate, acod)], on, S.rac)
+        send((*scod, on, S.rs))
+        send((*spln, on, S.rs))
+        if mate == root:
+            acs, aps = ne, nr
+            g.wait_ge(S.rac, acs)
+            send((acod, [(c, acod) for c in peers[NEAR:]], off, S.rac))
+        elif die == topo.die(root):
+            acs = aps = ne
+            if from_root <= NEAR:
+                g.wait_ge(S.rac, acs)
+                send((acod, [(mate, acod)], on, S.rac))
+        else:
+            acs, aps = nn if from_root <= NEAR else ne, ne
 
-    g.tensor.wait_ge(S.lw, 32)
-    g.tensor.wait_ge(S.qs, ngive)
-    g.tensor.wait_ge(S.qt, 1)
-    g.tensor.wait_ge(S.rs, ne + nr if mate == root else 2 * nn)
-    for b in range(4):
-        g.tensor.matmul_mx(T.pd[:, 512 * b:512 * b + NT], T.sc[:, b * NT:(b + 1) * NT], T.sp[:, b * NT:(b + 1) * NT],
-                           T.wqc[:], T.wqp[:], True, True).then_inc(S.dd, 1)
-    g.tensor.wait_ge(S.qb, 1)
-    if is_root:
-        g.tensor.wait_ge(S.qa, 1)
-    else:
-        g.tensor.wait_ge(S.rap, nr if mate == root else ne)
-        g.tensor.wait_ge(S.rac, nr if mate == root else ne if die == topo.die(root) else nn)
-    for b in range(4):
-        g.tensor.matmul_mx(T.pm[:, 512 * b:512 * b + NT], T.bc[:, b * NT:(b + 1) * NT], T.bp[:, b * NT:(b + 1) * NT],
-                           T.ac[:], T.ap[:], True, True).then_inc(S.mm, 1)
+    def products_d():
+        g.tensor.wait_ge(S.lw, 32)
+        g.tensor.wait_ge(S.qs, 1)
+        g.tensor.wait_ge(S.qt, 1)
+        g.tensor.wait_ge(S.rs, 2 * ne + (ne + nr if mate == root else 2 * nn))
+        for b in range(4):
+            g.tensor.matmul_mx(T.pd[:, 512 * b:512 * b + NT], T.sc[:, b * NT:(b + 1) * NT],
+                               T.sp[:, b * NT:(b + 1) * NT], T.wqc[:], T.wqp[:], True, True).then_inc(S.dd, 1)
+
+    def products_a():
+        g.tensor.wait_ge(S.qb, 1)
+        if is_root:
+            g.tensor.wait_ge(S.qa, 1)
+        else:
+            g.tensor.wait_ge(S.rac, acs)
+            g.tensor.wait_ge(S.rap, aps)
+        for b in range(4):
+            g.tensor.matmul_mx(T.pm[:, 512 * b:512 * b + NT], T.bc[:, b * NT:(b + 1) * NT],
+                               T.bp[:, b * NT:(b + 1) * NT], T.ac[:], T.ap[:], True, True).then_inc(S.mm, 1)
+
+    for f in (products_d, products_a) if from_root else (products_a, products_d):
+        f()
 
     g.vector.wait_ge(S.dd, 4)
     for b in range(4):
@@ -167,53 +212,57 @@ def rank_program(g, core, T, topo):
     g.vector.quantize_mx(T.xc[:], T.xp[:], T.tx[:]).then_inc(S.qx, 1)
 
     g.wait_ge(S.qv, 1)
-    send(vcod(OWN), [(c, vcod(slot_at(c))) for c in peers], off, S["rc%d" % k])
-    send(vpln(OWN), [(c, vpln(slot_at(c))) for c in peers], off, S["rp%d" % k])
-    send(vcod(OWN), [(mate, vcod(MATE))], rest, S.rm)
-    send(vpln(OWN), [(mate, vpln(MATE))], rest, S.rm)
-    far = [(k + 1 + i) % len(chips) for i in range(OFF)]
-    for i in range(OFF):
-        g.wait_ge(S["rc%d" % far[i]], ne)
-    send(vcod(0, OFF), [(mate, vcod(FWD, OFF))], on, S.rf)
-    for i in range(OFF):
-        g.wait_ge(S["rp%d" % far[i]], ne)
-    send(vpln(0, OFF), [(mate, vpln(FWD, OFF))], on, S.rf)
+    send((vcod(OWN), to(vcod, peers[:NEAR]), off, rc),
+         (vcod(OWN), [(helper(core), vcod(OWN)), (mate, vcod(MATE))], rest, S.rmc))
+    send((vpln(OWN), to(vpln, peers[:NEAR]), off, rp),
+         (vpln(OWN), [(helper(core), vpln(OWN)), (mate, vpln(MATE))], rest, S.rmp))
+    for gi, (lo, n) in enumerate(GROUPS):
+        for s, view in (("rc", vcod), ("rp", vpln)):
+            for c in peers[lo:lo + n]:
+                g.wait_ge(S["%s%d" % (s, T.rank_of(c))], ne)
+            send((view(lo, n), [(mate, view(FWD + lo, n))], on, S["rf%d" % gi]))
 
+    order = [(0, OWN, core, [(S.qv, 1)]), (2, MATE, mate, [(S.rmc, nr), (S.rmp, nr)])]
+    for gi, (lo, n) in enumerate(GROUPS):
+        for i in range(lo, lo + n):
+            early = 4 if topo.chip(peers[i]) == topo.chip(root) else 0
+            j = T.rank_of(peers[i])
+            order.append((6 + gi - early, i, peers[i], [(S["rc%d" % j], ne), (S["rp%d" % j], ne)]))
+            order.append((8 + 2 * gi, FWD + i, cross[i], [(S["rf%d" % gi], 2 * nn)]))
+    order.sort(key=lambda o: o[0])
     g.tensor.wait_ge(S.qx, 1)
-    order = [(OWN, core, [(S.qv, 1)]), (MATE, mate, [(S.rm, 2 * nr)])]
-    order += [(i, peers[i], [(S["rc%d" % far[i]], ne), (S["rp%d" % far[i]], ne)]) for i in range(OFF)]
-    order += [(FWD + i, cross[i], [(S.rf, 2 * nn)]) for i in range(OFF)]
-    nv = na = nst = nss = 0
-    for n, (slot, src, sems) in enumerate(order):
+    nm = nv = na = nst = 0
+    for n, (_, slot, src, sems) in enumerate(order):
         j = T.rank_of(src)
-        bank = (T.pm if n % 8 < 4 else T.pd)[:, 512 * (n % 4):512 * (n % 4) + NX]
-        if n >= 8:
-            g.tensor.wait_ge(S.cv if n % 2 == 0 else S.ca, (n - 8) // 2 + 1)
         for s, v in sems:
             g.tensor.wait_ge(s, v)
-        g.tensor.matmul_mx(bank, T.vc[:, slot * NT:(slot + 1) * NT], T.vp[:, slot * NT:(slot + 1) * NT],
-                           T.xc[:], T.xp[:], True, True).then_inc(S.my, 1)
-        dst = T.ysb[:, NX * j:NX * (j + 1)]
-        if n % 2 == 0:
-            g.vector.wait_ge(S.my, n + 1)
-            g.vector.tensor_copy(dst, bank).then_inc(S.cv, 1)
-            nv += 1
-            done = (S.cv, nv)
-        else:
-            g.scalar.wait_ge(S.my, n + 1)
-            g.scalar.activation(dst, bank, ActivationFunctionType.Copy).then_inc(S.ca, 1)
-            na += 1
-            done = (S.ca, na)
-        if n == N - 1:
-            g.scalar.wait_ge(*done)
-            g.scalar.dma_start(T.y[:, NX * j:NX * (j + 1)], dst).then_inc(S.ss, 16)
-            nss += 16
-        else:
-            g.sync.wait_ge(*done)
-            g.sync.dma_start(T.y[:, NX * j:NX * (j + 1)], dst).then_inc(S.st, 16)
-            nst += 16
-    g.scalar.wait_ge(S.ss, nss)
+        halves = 1 if n < N - 2 else 2
+        w = NX // halves
+        for h in range(halves):
+            bank = n if halves == 1 else 2 * (n - N + 2) + h
+            if halves == 2:
+                g.tensor.wait_ge(S.cv if h == 0 else S.ca, n - N + 3)
+            out = (T.pm if bank < 4 else T.pd)[:, 512 * (bank % 4):512 * (bank % 4) + w]
+            g.tensor.matmul_mx(out, T.vc[:, slot * NT:(slot + 1) * NT], T.vp[:, slot * NT:(slot + 1) * NT],
+                               T.xc[:, h * w:(h + 1) * w], T.xp[:, h * w:(h + 1) * w], True, True).then_inc(S.my, 1)
+            nm += 1
+            dst = T.ysb[:, NX * j + h * w:NX * j + (h + 1) * w]
+            if (n if halves == 1 else h) % 2 == 0:
+                g.vector.wait_ge(S.my, nm)
+                g.vector.tensor_copy(dst, out).then_inc(S.cv, 1)
+                nv += 1
+            else:
+                g.scalar.wait_ge(S.my, nm)
+                g.scalar.activation(dst, out, ActivationFunctionType.Copy).then_inc(S.ca, 1)
+                na += 1
+        last = n == N - 1
+        q = g.scalar if last else g.sync
+        if halves == 2 or n % 2 == 0:
+            q.wait_ge(S.cv, nv)
+        if halves == 2 or n % 2 == 1:
+            q.wait_ge(S.ca, na)
+        q.dma_start(T.y[:, NX * j:NX * (j + 1)], T.ysb[:, NX * j:NX * (j + 1)]).then_inc(S.ss if last else S.st, 16)
+        nst += 0 if last else 16
+    g.scalar.wait_ge(S.ss, 16)
     g.sync.wait_ge(S.st, nst)
     g.wait_ge(S.sent, sent[0])
-    if is_root:
-        g.wait_ge(S.sa, 2 * ne)

from concourse.bass import DstId, RemoteDMATransfer
from concourse.mybir import dt, AluOpType, ActivationFunctionType

NT, NX, N = 128, 384, 10
C = 0.043
OFF = 4
NEAR = 2
OWN, FWD, MATE = OFF, OFF + 1, 2 * OFF + 1
GROUPS = [(OFF - NEAR, NEAR), (0, OFF - NEAR)]
GIVE_ROOT, GIVE_OTHER, GIVE_HELPER, KEEP = 3, 0, 1, 2
F8, U8, BF, F32 = "float8_e4m3fn_x4", "uint8", "bfloat16", "float32"

SCRATCH = {
    "ta": ("sbuf", [128, 4 * NT], BF),
    "tb": ("sbuf", [128, 16 * NT], BF),
    "tx": ("sbuf", [128, 4 * NX], BF),
    "ones": ("sbuf", [128, NT], BF),
    "eye": ("sbuf", [128, NT], BF),
    "diag": ("sbuf", [128, 4 * NT + 4], BF),
    "tmp": ("sbuf", [128, 4 * NT], F32),
    "tv": ("sbuf", [128, 4 * NT], BF),
    "ysb": ("sbuf", [128, N * NX], F32),
    "ac": ("sbuf", [128, NT], F8), "ap": ("sbuf", [128, NT], U8),
    "bc": ("sbuf", [128, 4 * NT], F8), "bp": ("sbuf", [128, 4 * NT], U8),
    "xc": ("sbuf", [128, NX], F8), "xp": ("sbuf", [128, NX], U8),
    "sc": ("sbuf", [128, 4 * NT], F8), "sp": ("sbuf", [128, 4 * NT], U8),
    "wqc": ("sbuf", [128, NT], F8), "wqp": ("sbuf", [128, NT], U8),
    "vc": ("sbuf", [128, N * NT], F8), "vp": ("sbuf", [128, N * NT], U8),
    "pd": ("psum", [128, 2048], F32),
    "pm": ("psum", [128, 2048], F32),
}
SEMAPHORES = ["la", "lb", "lx", "lw", "one", "zero", "dia", "cp", "qa", "qb", "qs", "qt", "qx", "dd", "mm", "ml", "ad",
              "qv", "sent", "rs", "rac", "rap", "rmc", "rmp", "rf0", "rf1", "my", "cv", "ca", "st", "ss"]
SEMAPHORES += ["%s%d" % (s, j) for s in ("rc", "rp") for j in range(N)]


def _bits(m):
    return bin(m).count("1")


def rank_program(g, core, T, topo):
    S = T.sem
    cores = list(T.cores)
    chips = sorted(set(topo.chip(c) for c in cores))
    if topo.chip(core) not in chips:
        return

    def at(k, die):
        ch = chips[k % len(chips)]
        return [c for c in cores if topo.chip(c) == ch and topo.die(c) == die][0]

    def helper(c):
        return [h for h in range(topo.CHIPS * topo.CORES_PER_CHIP)
                if topo.chip(h) == topo.chip(c) and topo.die(h) == topo.die(c) and h not in cores][0]

    k = chips.index(topo.chip(core))
    die = topo.die(core)
    me = at(k, die)
    if core != me and core != helper(me):
        return
    root = cores[T.root]
    is_root = core == root
    mate = [c for c in cores if topo.chip(c) == topo.chip(core) and c != me][0]
    peers = [at(k + 1 + i, die) for i in range(OFF)]
    cross = [at(k + 1 + i, topo.die(mate)) for i in range(OFF)]
    off = topo.mask(core, peers[0])
    on = topo.mask(core, mate)
    rest = on & ~off
    ne, nr, nn = _bits(off), _bits(rest), _bits(on)
    from_root = (k - chips.index(topo.chip(root))) % len(chips)
    sent = [0]

    def slot_at(c, dst):
        i = (chips.index(topo.chip(c)) - chips.index(topo.chip(dst)) - 1) % len(chips)
        return i if topo.die(c) == topo.die(dst) else FWD + i

    def send(*parts):
        transfers = []
        for src, dsts, mask, sem in parts:
            ids = []
            for c, _ in dsts:
                rid, pid, _e = topo.addr(c)
                ids.append(DstId(rid=rid, pnc=pid))
            transfers.append(RemoteDMATransfer(dst_ids=ids, dma_engine_mask=mask, remote_sem=sem, srcs=[src],
                                               dsts=[d for _, d in dsts]))
            sent[0] += _bits(mask)
        g.remote_dma_fused(transfers, local_sem=S.sent)

    def vcod(a, n=1):
        return T.vc[:, a * NT:(a + n) * NT].bitcast(dt.uint8)

    def vpln(a, n=1):
        return T.vp[:, a * NT:(a + n) * NT]

    def to(view, cs):
        return [(c, view(slot_at(me, c))) for c in cs]

    acod = T.ac[:].bitcast(dt.uint8)
    apln = T.ap[:]
    rc, rp = S["rc%d" % T.rank_of(me)], S["rp%d" % T.rank_of(me)]

    if core == me:
        if is_root:
            g.sync.dma_start(T.ta[:], T.a[:]).then_inc(S.la, 16)
        q = g.sync if is_root else g.scalar
        q.dma_start(T.wqc[:].bitcast(dt.uint8), T.wc[:]).then_inc(S.lw, 16)
        q.dma_start(T.wqp[:], T.ws[:]).then_inc(S.lw, 16)
        g.sync.dma_start(T.tb[:], T.bb[:]).then_inc(S.lb, 16)
        if is_root:
            g.sync.wait_ge(S.qb, 1)
        g.sync.dma_start(T.tx[:], T.x[:]).then_inc(S.lx, 16)

    g.vector.memset(T.ones[:], 1.0).then_inc(S.one, 1)
    g.vector.memset(T.diag[:], 0.0).then_inc(S.zero, 1)
    g.wait_ge(S.one, 1)
    g.affine_select(T.eye[:], T.ones[:], [[-1, NT]], AluOpType.is_equal, 0.0, 0, 1).then_inc(S.dia, 1)
    g.vector.wait_ge(S.zero, 1)
    g.vector.wait_ge(S.dia, 1)
    g.vector.tensor_copy(T.diag[:, 3:4 * NT:4], T.eye[:]).then_inc(S.cp, 1)
    g.vector.wait_ge(S.cp, 1)

    def pick(b, sem):
        g.vector.quantize_mx(T.sc[:, b * NT:(b + 1) * NT], T.sp[:, b * NT:(b + 1) * NT],
                             T.diag[:, 3 - b:3 - b + 4 * NT]).then_inc(sem, 1)

    give = GIVE_HELPER if core != me else GIVE_ROOT if die == topo.die(root) else GIVE_OTHER
    taker = me if core != me else mate
    pick(give, S.qs)
    mine = slice(give * NT, (give + 1) * NT)
    scod = (T.sc[:, mine].bitcast(dt.uint8), [(taker, T.sc[:, mine].bitcast(dt.uint8))])
    spln = (T.sp[:, mine], [(taker, T.sp[:, mine])])
    g.wait_ge(S.qs, 1)

    if core != me:
        send((*scod, off, S.rs))
        send((*spln, off, S.rs))
        if not from_root:
            g.wait_ge(S.rap, ne)
            send((apln, [(c, apln) for c in peers], off, S.rap))
        g.wait_ge(S.rmc, nr)
        send((vcod(OWN), to(vcod, peers[NEAR:]), off, rc))
        g.wait_ge(S.rmp, nr)
        send((vpln(OWN), to(vpln, peers[NEAR:]), off, rp))
        g.wait_ge(S.sent, sent[0])
        return

    if is_root:
        g.vector.wait_ge(S.la, 16)
        g.vector.quantize_mx(T.ac[:], T.ap[:], T.ta[:]).then_inc(S.qa, 1)
    pick(KEEP, S.qt)
    g.vector.wait_ge(S.lb, 16)
    g.vector.quantize_mx(T.bc[:], T.bp[:], T.tb[:]).then_inc(S.qb, 1)

    acs = aps = 0
    if is_root:
        send((*spln, off, S.rs))
        g.wait_ge(S.qa, 1)
        send((apln, [(helper(c), apln) for c in (mate, core)], off, S.rap))
        send((acod, [(c, acod) for c in [mate] + peers[:NEAR]], off, S.rac))
        send((acod, [(c, acod) for c in peers[NEAR:]], off, S.rac))
        send((apln, [(mate, apln)], rest, S.rap))
        send((*scod, rest, S.rs))
    else:
        send((*scod, on, S.rs))
        send((*spln, on, S.rs))
        if mate == root:
            acs, aps = ne, nr
            g.wait_ge(S.rac, acs)
            send((acod, [(c, acod) for c in peers[NEAR:]], off, S.rac))
        elif die == topo.die(root):
            acs = aps = ne
            if from_root <= NEAR:
                g.wait_ge(S.rac, acs)
                send((acod, [(mate, acod)], on, S.rac))
        else:
            acs, aps = nn if from_root <= NEAR else ne, ne

    def products_d():
        g.tensor.wait_ge(S.lw, 32)
        g.tensor.wait_ge(S.qs, 1)
        g.tensor.wait_ge(S.qt, 1)
        g.tensor.wait_ge(S.rs, 2 * ne + (ne + nr if mate == root else 2 * nn))
        for b in range(4):
            g.tensor.matmul_mx(T.pd[:, 512 * b:512 * b + NT], T.sc[:, b * NT:(b + 1) * NT],
                               T.sp[:, b * NT:(b + 1) * NT], T.wqc[:], T.wqp[:], True, True).then_inc(S.dd, 1)

    def products_a():
        g.tensor.wait_ge(S.qb, 1)
        if is_root:
            g.tensor.wait_ge(S.qa, 1)
        else:
            g.tensor.wait_ge(S.rac, acs)
            g.tensor.wait_ge(S.rap, aps)
        for b in range(4):
            g.tensor.matmul_mx(T.pm[:, 512 * b:512 * b + NT], T.bc[:, b * NT:(b + 1) * NT],
                               T.bp[:, b * NT:(b + 1) * NT], T.ac[:], T.ap[:], True, True).then_inc(S.mm, 1)

    for f in (products_d, products_a) if from_root else (products_a, products_d):
        f()

    g.vector.wait_ge(S.dd, 4)
    for b in range(4):
        g.scalar.wait_ge(S.mm, b + 1)
        g.scalar.activation(T.tmp[:, b * NT:(b + 1) * NT], T.pm[:, 512 * b:512 * b + NT],
                            ActivationFunctionType.Copy, scale=C).then_inc(S.ml, 1)
        g.vector.wait_ge(S.ml, b + 1)
        g.vector.tensor_tensor(T.tv[:, b:4 * NT:4], T.tmp[:, b * NT:(b + 1) * NT], T.pd[:, 512 * b:512 * b + NT],
                               AluOpType.add).then_inc(S.ad, 1)
    g.vector.wait_ge(S.ad, 4)
    g.vector.quantize_mx(T.vc[:, OWN * NT:(OWN + 1) * NT], T.vp[:, OWN * NT:(OWN + 1) * NT], T.tv[:]).then_inc(S.qv, 1)
    g.vector.wait_ge(S.lx, 16)
    g.vector.quantize_mx(T.xc[:], T.xp[:], T.tx[:]).then_inc(S.qx, 1)

    g.wait_ge(S.qv, 1)
    send((vcod(OWN), to(vcod, peers[:NEAR]), off, rc),
         (vcod(OWN), [(helper(core), vcod(OWN)), (mate, vcod(MATE))], rest, S.rmc))
    send((vpln(OWN), to(vpln, peers[:NEAR]), off, rp),
         (vpln(OWN), [(helper(core), vpln(OWN)), (mate, vpln(MATE))], rest, S.rmp))
    for gi, (lo, n) in enumerate(GROUPS):
        for s, view in (("rc", vcod), ("rp", vpln)):
            for c in peers[lo:lo + n]:
                g.wait_ge(S["%s%d" % (s, T.rank_of(c))], ne)
            send((view(lo, n), [(mate, view(FWD + lo, n))], on, S["rf%d" % gi]))

    order = [(0, OWN, core, [(S.qv, 1)]), (2, MATE, mate, [(S.rmc, nr), (S.rmp, nr)])]
    for gi, (lo, n) in enumerate(GROUPS):
        for i in range(lo, lo + n):
            early = 4 if topo.chip(peers[i]) == topo.chip(root) else 0
            j = T.rank_of(peers[i])
            order.append((6 + gi - early, i, peers[i], [(S["rc%d" % j], ne), (S["rp%d" % j], ne)]))
            order.append((8 + 2 * gi, FWD + i, cross[i], [(S["rf%d" % gi], 2 * nn)]))
    order.sort(key=lambda o: o[0])
    g.tensor.wait_ge(S.qx, 1)
    nm = nv = na = nst = 0
    for n, (_, slot, src, sems) in enumerate(order):
        j = T.rank_of(src)
        for s, v in sems:
            g.tensor.wait_ge(s, v)
        halves = 1 if n < N - 2 else 2
        w = NX // halves
        for h in range(halves):
            bank = n if halves == 1 else 2 * (n - N + 2) + h
            if halves == 2:
                g.tensor.wait_ge(S.cv if h == 0 else S.ca, n - N + 3)
            out = (T.pm if bank < 4 else T.pd)[:, 512 * (bank % 4):512 * (bank % 4) + w]
            g.tensor.matmul_mx(out, T.vc[:, slot * NT:(slot + 1) * NT], T.vp[:, slot * NT:(slot + 1) * NT],
                               T.xc[:, h * w:(h + 1) * w], T.xp[:, h * w:(h + 1) * w], True, True).then_inc(S.my, 1)
            nm += 1
            dst = T.ysb[:, NX * j + h * w:NX * j + (h + 1) * w]
            if (n if halves == 1 else h) % 2 == 0:
                g.vector.wait_ge(S.my, nm)
                g.vector.tensor_copy(dst, out).then_inc(S.cv, 1)
                nv += 1
            else:
                g.scalar.wait_ge(S.my, nm)
                g.scalar.activation(dst, out, ActivationFunctionType.Copy).then_inc(S.ca, 1)
                na += 1
        last = n == N - 1
        q = g.scalar if last else g.sync
        if halves == 2 or n % 2 == 0:
            q.wait_ge(S.cv, nv)
        if halves == 2 or n % 2 == 1:
            q.wait_ge(S.ca, na)
        q.dma_start(T.y[:, NX * j:NX * (j + 1)], T.ysb[:, NX * j:NX * (j + 1)]).then_inc(S.ss if last else S.st, 16)
        nst += 0 if last else 16
    g.scalar.wait_ge(S.ss, 16)
    g.sync.wait_ge(S.st, nst)
    g.wait_ge(S.sent, sent[0])
